import numpy as np
import ml_dtypes

BF16 = ml_dtypes.bfloat16


def bf(x):
    return np.asarray(x, np.float32).astype(BF16)


def f32(x):
    return np.asarray(x, np.float32)


def f64(x):
    return np.asarray(x).astype(np.float64)


def striped(idx):
    return np.tile(idx.reshape(-1, 16).T, (8, 1))


S, K, M, N = 512, 128, 512, 128


def setup_inputs():
    return {"base": bf(np.random.standard_normal((M, S))), "x": bf(np.random.standard_normal((K, N))), "w": bf(np.random.standard_normal((K, M)) / np.sqrt(K)), "s": f32(0.5 + np.random.random_sample((M, 1))), "b": f32(0.5 * np.random.standard_normal((M, 1))), "offs": striped(np.random.permutation(S)[:N])}


def reference(base, x, w, s, b, offs):
    idx = offs[:16].T.reshape(-1)
    z = f64(base).copy()
    z[:, idx] = f64(w).T @ f64(x)
    return z * f64(s) + f64(b)

@@ -1,0 +1,69 @@
+import concourse.mybir as mybir
+from concourse.masks import make_identity
+
+BF16, F32, U16 = mybir.dt.bfloat16, mybir.dt.float32, mybir.dt.uint16
+MULT, ADD = mybir.AluOpType.mult, mybir.AluOpType.add
+IDENTITY = mybir.ActivationFunctionType.Identity
+
+P = 128
+S = 512
+M = 512
+N = 128
+BLOCKS = M // P
+
+FLOPS = 2 * P * M * N
+
+
+def tile_scatter_matmul_kernel(tc, base, x, w, s, b, offs, out):
+    nc = tc.nc
+    with (
+        tc.tile_pool(name="held", bufs=1) as held,
+        tc.psum_pool(name="windows", bufs=1) as windows,
+    ):
+        offsets = held.tile([P, N // 16], U16, name="offsets")
+        nc.sync.dma_start(offsets[:], offs)
+
+        ident = held.tile([P, P], BF16, name="ident")
+        make_identity(nc, ident[:])
+
+        base_tiles = [held.tile([P, S], BF16, name=f"base{a}") for a in range(BLOCKS)]
+        for a in range(BLOCKS):
+            queue = nc.sync if a % 2 == 0 else nc.scalar
+            queue.dma_start(base_tiles[a][:], base[a * P : (a + 1) * P, :])
+
+        x_tile = held.tile([P, N], BF16, name="x_tile")
+        nc.gpsimd.dma_start(x_tile[:], x)
+        w_tile = held.tile([P, M], BF16, name="w_tile")
+        nc.gpsimd.dma_start(w_tile[:], w)
+
+        gain = held.tile([P, BLOCKS], F32, name="gain")
+        shift = held.tile([P, BLOCKS], F32, name="shift")
+        with nc.allow_non_contiguous_dma(reason="one float32 to a partition for each block"):
+            nc.sync.dma_start(gain[:], s.rearrange("(a p) o -> p (a o)", p=P))
+            nc.scalar.dma_start(shift[:], b.rearrange("(a p) o -> p (a o)", p=P))
+
+        window_tiles = [windows.tile([P, S], F32, name=f"window{a}") for a in range(BLOCKS)]
+        for a in range(BLOCKS):
+            nc.tensor.matmul(window_tiles[a][:], ident[:], base_tiles[a][:], start=True, stop=True)
+
+        for a in range(BLOCKS):
+            nc.tensor.matmul(
+                window_tiles[a][:].indirect(offsets[:]),
+                w_tile[:, a * P : (a + 1) * P],
+                x_tile[:],
+                start=True,
+                stop=True,
+            )
+
+        for a in range(BLOCKS):
+            result = held.tile([P, S], F32, name=f"result{a}")
+            if a % 2 == 0:
+                nc.vector.tensor_scalar(
+                    result[:], window_tiles[a][:], gain[:, a : a + 1], shift[:, a : a + 1], MULT, ADD
+                )
+                nc.sync.dma_start(out[a * P : (a + 1) * P, :], result[:])
+            else:
+                nc.scalar.activation(
+                    result[:], window_tiles[a][:], IDENTITY, bias=shift[:, a : a + 1], scale=gain[:, a : a + 1]
+                )
+                nc.scalar.dma_start(out[a * P : (a + 1) * P, :], result[:])

@@ -20,27 +20,26 @@ def tile_scatter_matmul_kernel(tc, base, x, w, s, b, offs, out):
         tc.tile_pool(name="held", bufs=1) as held,
         tc.psum_pool(name="windows", bufs=1) as windows,
     ):
-        offsets = held.tile([P, N // 16], U16, name="offsets")
-        nc.sync.dma_start(offsets[:], offs)
-
-        ident = held.tile([P, P], BF16, name="ident")
-        make_identity(nc, ident[:])
-
         base_tiles = [held.tile([P, S], BF16, name=f"base{a}") for a in range(BLOCKS)]
         for a in range(BLOCKS):
             queue = nc.sync if a % 2 == 0 else nc.scalar
             queue.dma_start(base_tiles[a][:], base[a * P : (a + 1) * P, :])
 
+        offsets = held.tile([P, N // 16], U16, name="offsets")
+        nc.sync.dma_start(offsets[:], offs)
         x_tile = held.tile([P, N], BF16, name="x_tile")
-        nc.gpsimd.dma_start(x_tile[:], x)
+        nc.sync.dma_start(x_tile[:], x)
         w_tile = held.tile([P, M], BF16, name="w_tile")
-        nc.gpsimd.dma_start(w_tile[:], w)
+        nc.scalar.dma_start(w_tile[:], w)
+
+        ident = held.tile([P, P], BF16, name="ident")
+        make_identity(nc, ident[:])
 
         gain = held.tile([P, BLOCKS], F32, name="gain")
         shift = held.tile([P, BLOCKS], F32, name="shift")
         with nc.allow_non_contiguous_dma(reason="one float32 to a partition for each block"):
-            nc.sync.dma_start(gain[:], s.rearrange("(a p) o -> p (a o)", p=P))
-            nc.scalar.dma_start(shift[:], b.rearrange("(a p) o -> p (a o)", p=P))
+            nc.gpsimd.dma_start(gain[:], s.rearrange("(a p) o -> p (a o)", p=P))
+            nc.gpsimd.dma_start(shift[:], b.rearrange("(a p) o -> p (a o)", p=P))
 
         window_tiles = [windows.tile([P, S], F32, name=f"window{a}") for a in range(BLOCKS)]
         for a in range(BLOCKS):

@@ -32,14 +32,19 @@ def tile_scatter_matmul_kernel(tc, base, x, w, s, b, offs, out):
         w_tile = held.tile([P, M], BF16, name="w_tile")
         nc.scalar.dma_start(w_tile[:], w)
 
-        ident = held.tile([P, P], BF16, name="ident")
-        make_identity(nc, ident[:])
-
         gain = held.tile([P, BLOCKS], F32, name="gain")
         shift = held.tile([P, BLOCKS], F32, name="shift")
         with nc.allow_non_contiguous_dma(reason="one float32 to a partition for each block"):
-            nc.gpsimd.dma_start(gain[:], s.rearrange("(a p) o -> p (a o)", p=P))
-            nc.gpsimd.dma_start(shift[:], b.rearrange("(a p) o -> p (a o)", p=P))
+            nc.sync.dma_start(gain[:], s.rearrange("(a p) o -> p (a o)", p=P))
+            nc.scalar.dma_start(shift[:], b.rearrange("(a p) o -> p (a o)", p=P))
+
+        ident = held.tile([P, P], BF16, name="ident")
+        make_identity(nc, ident[:])
+
+        one_column = held.tile([P, 1], F32, name="one_column")
+        nc.vector.memset(one_column[:], 0.0)
+        unread = held.tile([P, 1], F32, name="unread")
+        nc.scalar.activation(unread[:], one_column[:], IDENTITY)
 
         window_tiles = [windows.tile([P, S], F32, name=f"window{a}") for a in range(BLOCKS)]
         for a in range(BLOCKS):

@@ -10,6 +10,7 @@ S = 512
 M = 512
 N = 128
 BLOCKS = M // P
+WARM_MATMULS = 3
 
 FLOPS = 2 * P * M * N
 
@@ -20,6 +21,12 @@ def tile_scatter_matmul_kernel(tc, base, x, w, s, b, offs, out):
         tc.tile_pool(name="held", bufs=1) as held,
         tc.psum_pool(name="windows", bufs=1) as windows,
     ):
+        zeros = held.tile([P, S], BF16, name="zeros")
+        nc.vector.memset(zeros[:], 0.0)
+        unread_bank = windows.tile([P, S], F32, name="unread_bank")
+        for i in range(WARM_MATMULS):
+            nc.tensor.matmul(unread_bank[:], zeros[:, 0:P], zeros[:], start=True, stop=True)
+
         base_tiles = [held.tile([P, S], BF16, name=f"base{a}") for a in range(BLOCKS)]
         for a in range(BLOCKS):
             queue = nc.sync if a % 2 == 0 else nc.scalar

@@ -17,6 +17,8 @@ FLOPS = 2 * P * M * N
 
 def tile_scatter_matmul_kernel(tc, base, x, w, s, b, offs, out):
     nc = tc.nc
+    base_rows = base.rearrange("(p a) t -> p a t", a=BLOCKS)
+    out_rows = out.rearrange("(p a) t -> p a t", a=BLOCKS)
     with (
         tc.tile_pool(name="held", bufs=1) as held,
         tc.psum_pool(name="windows", bufs=1) as windows,
@@ -30,7 +32,7 @@ def tile_scatter_matmul_kernel(tc, base, x, w, s, b, offs, out):
         base_tiles = [held.tile([P, S], BF16, name=f"base{a}") for a in range(BLOCKS)]
         for a in range(BLOCKS):
             queue = nc.sync if a % 2 == 0 else nc.scalar
-            queue.dma_start(base_tiles[a][:], base[a * P : (a + 1) * P, :])
+            queue.dma_start(base_tiles[a][:], base_rows[:, a, :])
 
         offsets = held.tile([P, N // 16], U16, name="offsets")
         nc.sync.dma_start(offsets[:], offs)
@@ -41,9 +43,8 @@ def tile_scatter_matmul_kernel(tc, base, x, w, s, b, offs, out):
 
         gain = held.tile([P, BLOCKS], F32, name="gain")
         shift = held.tile([P, BLOCKS], F32, name="shift")
-        with nc.allow_non_contiguous_dma(reason="one float32 to a partition for each block"):
-            nc.sync.dma_start(gain[:], s.rearrange("(a p) o -> p (a o)", p=P))
-            nc.scalar.dma_start(shift[:], b.rearrange("(a p) o -> p (a o)", p=P))
+        nc.sync.dma_start(gain[:], s.rearrange("(p a) o -> p (a o)", a=BLOCKS))
+        nc.scalar.dma_start(shift[:], b.rearrange("(p a) o -> p (a o)", a=BLOCKS))
 
         ident = held.tile([P, P], BF16, name="ident")
         make_identity(nc, ident[:])
@@ -53,6 +54,10 @@ def tile_scatter_matmul_kernel(tc, base, x, w, s, b, offs, out):
         unread = held.tile([P, 1], F32, name="unread")
         nc.scalar.activation(unread[:], one_column[:], IDENTITY)
 
+        w_blocks = held.tile([P, BLOCKS, P], BF16, name="w_blocks")
+        for a in range(BLOCKS):
+            nc.vector.tensor_copy(w_blocks[:, a, :], w_tile[:, a:M:BLOCKS])
+
         window_tiles = [windows.tile([P, S], F32, name=f"window{a}") for a in range(BLOCKS)]
         for a in range(BLOCKS):
             nc.tensor.matmul(window_tiles[a][:], ident[:], base_tiles[a][:], start=True, stop=True)
@@ -60,7 +65,7 @@ def tile_scatter_matmul_kernel(tc, base, x, w, s, b, offs, out):
         for a in range(BLOCKS):
             nc.tensor.matmul(
                 window_tiles[a][:].indirect(offsets[:]),
-                w_tile[:, a * P : (a + 1) * P],
+                w_blocks[:, a, :],
                 x_tile[:],
                 start=True,
                 stop=True,
@@ -72,9 +77,9 @@ def tile_scatter_matmul_kernel(tc, base, x, w, s, b, offs, out):
                 nc.vector.tensor_scalar(
                     result[:], window_tiles[a][:], gain[:, a : a + 1], shift[:, a : a + 1], MULT, ADD
                 )
-                nc.sync.dma_start(out[a * P : (a + 1) * P, :], result[:])
+                nc.sync.dma_start(out_rows[:, a, :], result[:])
             else:
                 nc.scalar.activation(
                     result[:], window_tiles[a][:], IDENTITY, bias=shift[:, a : a + 1], scale=gain[:, a : a + 1]
                 )
-                nc.scalar.dma_start(out[a * P : (a + 1) * P, :], result[:])
+                nc.scalar.dma_start(out_rows[:, a, :], result[:])

@@ -30,16 +30,16 @@ def tile_scatter_matmul_kernel(tc, base, x, w, s, b, offs, out):
             nc.tensor.matmul(unread_bank[:], zeros[:, 0:P], zeros[:], start=True, stop=True)
 
         base_tiles = [held.tile([P, S], BF16, name=f"base{a}") for a in range(BLOCKS)]
-        for a in range(BLOCKS):
-            queue = nc.sync if a % 2 == 0 else nc.scalar
-            queue.dma_start(base_tiles[a][:], base_rows[:, a, :])
-
         offsets = held.tile([P, N // 16], U16, name="offsets")
-        nc.sync.dma_start(offsets[:], offs)
         x_tile = held.tile([P, N], BF16, name="x_tile")
-        nc.sync.dma_start(x_tile[:], x)
         w_tile = held.tile([P, M], BF16, name="w_tile")
+        nc.sync.dma_start(base_tiles[0][:], base_rows[:, 0, :])
+        nc.scalar.dma_start(base_tiles[1][:], base_rows[:, 1, :])
+        nc.sync.dma_start(base_tiles[2][:], base_rows[:, 2, :])
         nc.scalar.dma_start(w_tile[:], w)
+        nc.sync.dma_start(offsets[:], offs)
+        nc.scalar.dma_start(base_tiles[3][:], base_rows[:, 3, :])
+        nc.sync.dma_start(x_tile[:], x)
 
         gain = held.tile([P, BLOCKS], F32, name="gain")
         shift = held.tile([P, BLOCKS], F32, name="shift")

@@ -37,14 +37,14 @@ def tile_scatter_matmul_kernel(tc, base, x, w, s, b, offs, out):
         nc.scalar.dma_start(base_tiles[1][:], base_rows[:, 1, :])
         nc.sync.dma_start(base_tiles[2][:], base_rows[:, 2, :])
         nc.scalar.dma_start(w_tile[:], w)
+        nc.sync.dma_start(base_tiles[3][:], base_rows[:, 3, :])
         nc.sync.dma_start(offsets[:], offs)
-        nc.scalar.dma_start(base_tiles[3][:], base_rows[:, 3, :])
         nc.sync.dma_start(x_tile[:], x)
 
         gain = held.tile([P, BLOCKS], F32, name="gain")
         shift = held.tile([P, BLOCKS], F32, name="shift")
         nc.sync.dma_start(gain[:], s.rearrange("(p a) o -> p (a o)", a=BLOCKS))
-        nc.scalar.dma_start(shift[:], b.rearrange("(p a) o -> p (a o)", a=BLOCKS))
+        nc.sync.dma_start(shift[:], b.rearrange("(p a) o -> p (a o)", a=BLOCKS))
 
         ident = held.tile([P, P], BF16, name="ident")
         make_identity(nc, ident[:])

@@ -34,9 +34,9 @@ def tile_scatter_matmul_kernel(tc, base, x, w, s, b, offs, out):
         x_tile = held.tile([P, N], BF16, name="x_tile")
         w_tile = held.tile([P, M], BF16, name="w_tile")
         nc.sync.dma_start(base_tiles[0][:], base_rows[:, 0, :])
-        nc.scalar.dma_start(base_tiles[1][:], base_rows[:, 1, :])
+        nc.sync.dma_start(base_tiles[1][:], base_rows[:, 1, :])
+        nc.sync.dma_start(w_tile[:], w)
         nc.sync.dma_start(base_tiles[2][:], base_rows[:, 2, :])
-        nc.scalar.dma_start(w_tile[:], w)
         nc.sync.dma_start(base_tiles[3][:], base_rows[:, 3, :])
         nc.sync.dma_start(offsets[:], offs)
         nc.sync.dma_start(x_tile[:], x)

@@ -10,6 +10,7 @@ S = 512
 M = 512
 N = 128
 BLOCKS = M // P
+BURST = 256
 WARM_MATMULS = 3
 
 FLOPS = 2 * P * M * N
@@ -29,10 +30,10 @@ def tile_scatter_matmul_kernel(tc, base, x, w, s, b, offs, out):
         for i in range(WARM_MATMULS):
             nc.tensor.matmul(unread_bank[:], zeros[:, 0:P], zeros[:], start=True, stop=True)
 
-        base_tiles = [held.tile([P, S], BF16, name=f"base{a}") for a in range(BLOCKS)]
+        base_tiles = [held.tile([P, S], BF16, name=f"base{a}", align_bytes=BURST) for a in range(BLOCKS)]
         offsets = held.tile([P, N // 16], U16, name="offsets")
-        x_tile = held.tile([P, N], BF16, name="x_tile")
-        w_tile = held.tile([P, M], BF16, name="w_tile")
+        x_tile = held.tile([P, N], BF16, name="x_tile", align_bytes=BURST)
+        w_tile = held.tile([P, M], BF16, name="w_tile", align_bytes=BURST)
         nc.sync.dma_start(base_tiles[0][:], base_rows[:, 0, :])
         nc.sync.dma_start(base_tiles[1][:], base_rows[:, 1, :])
         nc.sync.dma_start(w_tile[:], w)
@@ -72,7 +73,7 @@ def tile_scatter_matmul_kernel(tc, base, x, w, s, b, offs, out):
             )
 
         for a in range(BLOCKS):
-            result = held.tile([P, S], F32, name=f"result{a}")
+            result = held.tile([P, S], F32, name=f"result{a}", align_bytes=BURST)
             if a % 2 == 0:
                 nc.vector.tensor_scalar(
                     result[:], window_tiles[a][:], gain[:, a : a + 1], shift[:, a : a + 1], MULT, ADD

@@ -12,6 +12,8 @@ N = 128
 BLOCKS = M // P
 BURST = 256
 WARM_MATMULS = 3
+EARLY = 1
+PIECE = 44
 
 FLOPS = 2 * P * M * N
 
@@ -34,11 +36,8 @@ def tile_scatter_matmul_kernel(tc, base, x, w, s, b, offs, out):
         offsets = held.tile([P, N // 16], U16, name="offsets")
         x_tile = held.tile([P, N], BF16, name="x_tile", align_bytes=BURST)
         w_tile = held.tile([P, M], BF16, name="w_tile", align_bytes=BURST)
-        nc.sync.dma_start(base_tiles[0][:], base_rows[:, 0, :])
-        nc.sync.dma_start(base_tiles[1][:], base_rows[:, 1, :])
         nc.sync.dma_start(w_tile[:], w)
-        nc.sync.dma_start(base_tiles[2][:], base_rows[:, 2, :])
-        nc.sync.dma_start(base_tiles[3][:], base_rows[:, 3, :])
+        nc.sync.dma_start(base_tiles[0][:], base_rows[:, 0, :])
         nc.sync.dma_start(offsets[:], offs)
         nc.sync.dma_start(x_tile[:], x)
 
@@ -46,6 +45,8 @@ def tile_scatter_matmul_kernel(tc, base, x, w, s, b, offs, out):
         shift = held.tile([P, BLOCKS], F32, name="shift")
         nc.sync.dma_start(gain[:], s.rearrange("(p a) o -> p (a o)", a=BLOCKS))
         nc.sync.dma_start(shift[:], b.rearrange("(p a) o -> p (a o)", a=BLOCKS))
+        for a in range(EARLY, BLOCKS):
+            nc.sync.dma_start(base_tiles[a][:], base_rows[:, a, :])
 
         ident = held.tile([P, P], BF16, name="ident")
         make_identity(nc, ident[:])
@@ -60,27 +61,39 @@ def tile_scatter_matmul_kernel(tc, base, x, w, s, b, offs, out):
             nc.vector.tensor_copy(w_blocks[:, a, :], w_tile[:, a:M:BLOCKS])
 
         window_tiles = [windows.tile([P, S], F32, name=f"window{a}") for a in range(BLOCKS)]
-        for a in range(BLOCKS):
-            nc.tensor.matmul(window_tiles[a][:], ident[:], base_tiles[a][:], start=True, stop=True)
 
-        for a in range(BLOCKS):
+        def fill(a, start, end):
             nc.tensor.matmul(
-                window_tiles[a][:].indirect(offsets[:]),
-                w_blocks[:, a, :],
-                x_tile[:],
-                start=True,
-                stop=True,
+                window_tiles[a][:, start:end], ident[:], base_tiles[a][:, start:end], start=True, stop=True
             )
 
-        for a in range(BLOCKS):
+        def scatter(a):
+            nc.tensor.matmul(
+                window_tiles[a][:].indirect(offsets[:]), w_blocks[:, a, :], x_tile[:], start=True, stop=True
+            )
+
+        def finish(a):
             result = held.tile([P, S], F32, name=f"result{a}", align_bytes=BURST)
             if a % 2 == 0:
-                nc.vector.tensor_scalar(
-                    result[:], window_tiles[a][:], gain[:, a : a + 1], shift[:, a : a + 1], MULT, ADD
-                )
-                nc.sync.dma_start(out_rows[:, a, :], result[:])
-            else:
                 nc.scalar.activation(
                     result[:], window_tiles[a][:], IDENTITY, bias=shift[:, a : a + 1], scale=gain[:, a : a + 1]
                 )
                 nc.scalar.dma_start(out_rows[:, a, :], result[:])
+            else:
+                nc.vector.tensor_scalar(
+                    result[:], window_tiles[a][:], gain[:, a : a + 1], shift[:, a : a + 1], MULT, ADD
+                )
+                nc.sync.dma_start(out_rows[:, a, :], result[:])
+
+        fill(0, 0, S)
+        scatter(0)
+        finish(0)
+
+        for a in (1, 2):
+            for start in range(0, S, PIECE):
+                fill(a, start, min(start + PIECE, S))
+        fill(3, 0, S)
+        for a in range(EARLY, BLOCKS):
+            scatter(a)
+        for a in range(EARLY, BLOCKS):
+            finish(a)

@@ -12,7 +12,7 @@ N = 128
 BLOCKS = M // P
 BURST = 256
 WARM_MATMULS = 3
-EARLY = 1
+EARLY = 2
 PIECE = 44
 
 FLOPS = 2 * P * M * N
@@ -36,8 +36,9 @@ def tile_scatter_matmul_kernel(tc, base, x, w, s, b, offs, out):
         offsets = held.tile([P, N // 16], U16, name="offsets")
         x_tile = held.tile([P, N], BF16, name="x_tile", align_bytes=BURST)
         w_tile = held.tile([P, M], BF16, name="w_tile", align_bytes=BURST)
-        nc.sync.dma_start(w_tile[:], w)
         nc.sync.dma_start(base_tiles[0][:], base_rows[:, 0, :])
+        nc.sync.dma_start(w_tile[:], w)
+        nc.sync.dma_start(base_tiles[1][:], base_rows[:, 1, :])
         nc.sync.dma_start(offsets[:], offs)
         nc.sync.dma_start(x_tile[:], x)
 
@@ -85,14 +86,16 @@ def tile_scatter_matmul_kernel(tc, base, x, w, s, b, offs, out):
                 )
                 nc.sync.dma_start(out_rows[:, a, :], result[:])
 
-        fill(0, 0, S)
-        scatter(0)
-        finish(0)
+        for a in range(EARLY):
+            fill(a, 0, S)
+        for a in range(EARLY):
+            scatter(a)
+        for a in range(EARLY):
+            finish(a)
 
-        for a in (1, 2):
+        for a in range(EARLY, BLOCKS):
             for start in range(0, S, PIECE):
                 fill(a, start, min(start + PIECE, S))
-        fill(3, 0, S)
         for a in range(EARLY, BLOCKS):
             scatter(a)
         for a in range(EARLY, BLOCKS):

@@ -10,9 +10,10 @@ S = 512
 M = 512
 N = 128
 BLOCKS = M // P
+HALVES = 2
+EACH = BLOCKS // HALVES
 BURST = 256
 WARM_MATMULS = 3
-EARLY = 2
 PIECE = 44
 
 FLOPS = 2 * P * M * N
@@ -20,8 +21,11 @@ FLOPS = 2 * P * M * N
 
 def tile_scatter_matmul_kernel(tc, base, x, w, s, b, offs, out):
     nc = tc.nc
-    base_rows = base.rearrange("(p a) t -> p a t", a=BLOCKS)
-    out_rows = out.rearrange("(p a) t -> p a t", a=BLOCKS)
+    base_rows = base.rearrange("(h p r) t -> p h r t", h=HALVES, r=EACH)
+    out_rows = out.rearrange("(h p r) t -> p h r t", h=HALVES, r=EACH)
+    s_rows = s.rearrange("(h p r) o -> p h (r o)", h=HALVES, r=EACH)
+    b_rows = b.rearrange("(h p r) o -> p h (r o)", h=HALVES, r=EACH)
+    w_halves = w.rearrange("k (h c) -> k h c", h=HALVES)
     with (
         tc.tile_pool(name="held", bufs=1) as held,
         tc.psum_pool(name="windows", bufs=1) as windows,
@@ -32,22 +36,20 @@ def tile_scatter_matmul_kernel(tc, base, x, w, s, b, offs, out):
         for i in range(WARM_MATMULS):
             nc.tensor.matmul(unread_bank[:], zeros[:, 0:P], zeros[:], start=True, stop=True)
 
-        base_tiles = [held.tile([P, S], BF16, name=f"base{a}", align_bytes=BURST) for a in range(BLOCKS)]
-        offsets = held.tile([P, N // 16], U16, name="offsets")
+        base_tiles = [held.tile([P, EACH, S], BF16, name=f"base_half{h}", align_bytes=BURST) for h in range(HALVES)]
+        w_tiles = [held.tile([P, EACH * P], BF16, name=f"w_half{h}", align_bytes=BURST) for h in range(HALVES)]
         x_tile = held.tile([P, N], BF16, name="x_tile", align_bytes=BURST)
-        w_tile = held.tile([P, M], BF16, name="w_tile", align_bytes=BURST)
-        nc.sync.dma_start(base_tiles[0][:], base_rows[:, 0, :])
-        nc.sync.dma_start(w_tile[:], w)
-        nc.sync.dma_start(base_tiles[1][:], base_rows[:, 1, :])
-        nc.sync.dma_start(offsets[:], offs)
-        nc.sync.dma_start(x_tile[:], x)
-
-        gain = held.tile([P, BLOCKS], F32, name="gain")
-        shift = held.tile([P, BLOCKS], F32, name="shift")
-        nc.sync.dma_start(gain[:], s.rearrange("(p a) o -> p (a o)", a=BLOCKS))
-        nc.sync.dma_start(shift[:], b.rearrange("(p a) o -> p (a o)", a=BLOCKS))
-        for a in range(EARLY, BLOCKS):
-            nc.sync.dma_start(base_tiles[a][:], base_rows[:, a, :])
+        offsets = held.tile([P, N // 16], U16, name="offsets")
+        gains = [held.tile([P, EACH], F32, name=f"gain{h}") for h in range(HALVES)]
+        shifts = [held.tile([P, EACH], F32, name=f"shift{h}") for h in range(HALVES)]
+        for h in range(HALVES):
+            nc.sync.dma_start(base_tiles[h][:], base_rows[:, h, :, :])
+            nc.sync.dma_start(w_tiles[h][:], w_halves[:, h, :])
+            if h == 0:
+                nc.sync.dma_start(offsets[:], offs)
+                nc.sync.dma_start(x_tile[:], x)
+            nc.sync.dma_start(gains[h][:], s_rows[:, h, :])
+            nc.sync.dma_start(shifts[h][:], b_rows[:, h, :])
 
         ident = held.tile([P, P], BF16, name="ident")
         make_identity(nc, ident[:])
@@ -57,46 +59,38 @@ def tile_scatter_matmul_kernel(tc, base, x, w, s, b, offs, out):
         unread = held.tile([P, 1], F32, name="unread")
         nc.scalar.activation(unread[:], one_column[:], IDENTITY)
 
-        w_blocks = held.tile([P, BLOCKS, P], BF16, name="w_blocks")
-        for a in range(BLOCKS):
-            nc.vector.tensor_copy(w_blocks[:, a, :], w_tile[:, a:M:BLOCKS])
+        w_blocks = [held.tile([P, EACH, P], BF16, name=f"w_blocks{h}") for h in range(HALVES)]
+        for h in range(HALVES):
+            nc.vector.tensor_copy(w_blocks[h][:], w_tiles[h][:].rearrange("k (c r) -> k r c", r=EACH))
 
         window_tiles = [windows.tile([P, S], F32, name=f"window{a}") for a in range(BLOCKS)]
 
-        def fill(a, start, end):
-            nc.tensor.matmul(
-                window_tiles[a][:, start:end], ident[:], base_tiles[a][:, start:end], start=True, stop=True
-            )
+        for h in range(HALVES):
+            width = S if h == 0 else PIECE
+            for r in range(EACH):
+                a = EACH * h + r
+                for start in range(0, S, width):
+                    end = min(start + width, S)
+                    nc.tensor.matmul(
+                        window_tiles[a][:, start:end], ident[:], base_tiles[h][:, r, start:end], start=True, stop=True
+                    )
 
-        def scatter(a):
-            nc.tensor.matmul(
-                window_tiles[a][:].indirect(offsets[:]), w_blocks[:, a, :], x_tile[:], start=True, stop=True
-            )
-
-        def finish(a):
-            result = held.tile([P, S], F32, name=f"result{a}", align_bytes=BURST)
-            if a % 2 == 0:
-                nc.scalar.activation(
-                    result[:], window_tiles[a][:], IDENTITY, bias=shift[:, a : a + 1], scale=gain[:, a : a + 1]
+            for r in range(EACH):
+                nc.tensor.matmul(
+                    window_tiles[EACH * h + r][:].indirect(offsets[:]),
+                    w_blocks[h][:, r, :],
+                    x_tile[:],
+                    start=True,
+                    stop=True,
                 )
-                nc.scalar.dma_start(out_rows[:, a, :], result[:])
-            else:
-                nc.vector.tensor_scalar(
-                    result[:], window_tiles[a][:], gain[:, a : a + 1], shift[:, a : a + 1], MULT, ADD
-                )
-                nc.sync.dma_start(out_rows[:, a, :], result[:])
 
-        for a in range(EARLY):
-            fill(a, 0, S)
-        for a in range(EARLY):
-            scatter(a)
-        for a in range(EARLY):
-            finish(a)
-
-        for a in range(EARLY, BLOCKS):
-            for start in range(0, S, PIECE):
-                fill(a, start, min(start + PIECE, S))
-        for a in range(EARLY, BLOCKS):
-            scatter(a)
-        for a in range(EARLY, BLOCKS):
-            finish(a)
+            for r in range(EACH):
+                a = EACH * h + r
+                gain, shift = gains[h][:, r : r + 1], shifts[h][:, r : r + 1]
+                result = held.tile([P, S], F32, name=f"result{a}", align_bytes=BURST)
+                if r == 0:
+                    nc.scalar.activation(result[:], window_tiles[a][:], IDENTITY, bias=shift, scale=gain)
+                    nc.scalar.dma_start(out_rows[:, h, r, :], result[:])
+                else:
+                    nc.vector.tensor_scalar(result[:], window_tiles[a][:], gain, shift, MULT, ADD)
+                    nc.sync.dma_start(out_rows[:, h, r, :], result[:])

@@ -43,7 +43,11 @@ def tile_scatter_matmul_kernel(tc, base, x, w, s, b, offs, out):
         gains = [held.tile([P, EACH], F32, name=f"gain{h}") for h in range(HALVES)]
         shifts = [held.tile([P, EACH], F32, name=f"shift{h}") for h in range(HALVES)]
         for h in range(HALVES):
-            nc.sync.dma_start(base_tiles[h][:], base_rows[:, h, :, :])
+            if h == 0:
+                for r in range(EACH):
+                    nc.sync.dma_start(base_tiles[h][:, r, :], base_rows[:, h, r, :])
+            else:
+                nc.sync.dma_start(base_tiles[h][:], base_rows[:, h, :, :])
             nc.sync.dma_start(w_tiles[h][:], w_halves[:, h, :])
             if h == 0:
                 nc.sync.dma_start(offsets[:], offs)

@@ -13,7 +13,7 @@ BLOCKS = M // P
 HALVES = 2
 EACH = BLOCKS // HALVES
 BURST = 256
-WARM_MATMULS = 3
+WARM_MATMULS = 12
 PIECE = 44
 
 FLOPS = 2 * P * M * N
@@ -21,39 +21,40 @@ FLOPS = 2 * P * M * N
 
 def tile_scatter_matmul_kernel(tc, base, x, w, s, b, offs, out):
     nc = tc.nc
-    base_rows = base.rearrange("(h p r) t -> p h r t", h=HALVES, r=EACH)
-    out_rows = out.rearrange("(h p r) t -> p h r t", h=HALVES, r=EACH)
-    s_rows = s.rearrange("(h p r) o -> p h (r o)", h=HALVES, r=EACH)
-    b_rows = b.rearrange("(h p r) o -> p h (r o)", h=HALVES, r=EACH)
-    w_halves = w.rearrange("k (h c) -> k h c", h=HALVES)
+    def rows_of_halves(tensor):
+        return (
+            tensor[0 : M // HALVES, :].rearrange("(p r) t -> p r t", r=EACH),
+            tensor[M // HALVES : M, :].rearrange("(r p) t -> p r t", r=EACH),
+        )
+
+    base_rows, out_rows, s_rows, b_rows = [rows_of_halves(tensor) for tensor in (base, out, s, b)]
     with (
         tc.tile_pool(name="held", bufs=1) as held,
         tc.psum_pool(name="windows", bufs=1) as windows,
     ):
-        zeros = held.tile([P, S], BF16, name="zeros")
+        zeros = held.tile([P, P], BF16, name="zeros")
         nc.vector.memset(zeros[:], 0.0)
-        unread_bank = windows.tile([P, S], F32, name="unread_bank")
+        unread_bank = windows.tile([P, P], F32, name="unread_bank")
         for i in range(WARM_MATMULS):
-            nc.tensor.matmul(unread_bank[:], zeros[:, 0:P], zeros[:], start=True, stop=True)
+            nc.tensor.matmul(unread_bank[:], zeros[:], zeros[:], start=True, stop=True)
 
         base_tiles = [held.tile([P, EACH, S], BF16, name=f"base_half{h}", align_bytes=BURST) for h in range(HALVES)]
         w_tiles = [held.tile([P, EACH * P], BF16, name=f"w_half{h}", align_bytes=BURST) for h in range(HALVES)]
         x_tile = held.tile([P, N], BF16, name="x_tile", align_bytes=BURST)
         offsets = held.tile([P, N // 16], U16, name="offsets")
-        gains = [held.tile([P, EACH], F32, name=f"gain{h}") for h in range(HALVES)]
-        shifts = [held.tile([P, EACH], F32, name=f"shift{h}") for h in range(HALVES)]
-        for h in range(HALVES):
-            if h == 0:
-                for r in range(EACH):
-                    nc.sync.dma_start(base_tiles[h][:, r, :], base_rows[:, h, r, :])
-            else:
-                nc.sync.dma_start(base_tiles[h][:], base_rows[:, h, :, :])
-            nc.sync.dma_start(w_tiles[h][:], w_halves[:, h, :])
-            if h == 0:
-                nc.sync.dma_start(offsets[:], offs)
-                nc.sync.dma_start(x_tile[:], x)
-            nc.sync.dma_start(gains[h][:], s_rows[:, h, :])
-            nc.sync.dma_start(shifts[h][:], b_rows[:, h, :])
+        gains = [held.tile([P, EACH, 1], F32, name=f"gain{h}") for h in range(HALVES)]
+        shifts = [held.tile([P, EACH, 1], F32, name=f"shift{h}") for h in range(HALVES)]
+        nc.sync.dma_start(base_tiles[0][:, 0, :], base_rows[0][:, 0, :])
+        nc.sync.dma_start(w_tiles[0][:], w[:, 0 : EACH * P])
+        nc.sync.dma_start(base_tiles[0][:, 1, :], base_rows[0][:, 1, :])
+        nc.sync.dma_start(offsets[:], offs)
+        nc.sync.dma_start(x_tile[:], x)
+        nc.sync.dma_start(gains[0][:], s_rows[0])
+        nc.sync.dma_start(shifts[0][:], b_rows[0])
+        nc.sync.dma_start(base_tiles[1][:], base_rows[1])
+        nc.sync.dma_start(w_tiles[1][:], w[:, EACH * P : M])
+        nc.sync.dma_start(gains[1][:], s_rows[1])
+        nc.sync.dma_start(shifts[1][:], b_rows[1])
 
         ident = held.tile([P, P], BF16, name="ident")
         make_identity(nc, ident[:])
@@ -63,9 +64,9 @@ def tile_scatter_matmul_kernel(tc, base, x, w, s, b, offs, out):
         unread = held.tile([P, 1], F32, name="unread")
         nc.scalar.activation(unread[:], one_column[:], IDENTITY)
 
-        w_blocks = [held.tile([P, EACH, P], BF16, name=f"w_blocks{h}") for h in range(HALVES)]
-        for h in range(HALVES):
-            nc.vector.tensor_copy(w_blocks[h][:], w_tiles[h][:].rearrange("k (c r) -> k r c", r=EACH))
+        w_regrouped = held.tile([P, EACH, P], BF16, name="w_regrouped")
+        nc.vector.tensor_copy(w_regrouped[:], w_tiles[0][:].rearrange("k (p r) -> k r p", r=EACH))
+        weights = (w_regrouped, w_tiles[1][:].rearrange("k (r p) -> k r p", r=EACH))
 
         window_tiles = [windows.tile([P, S], F32, name=f"window{a}") for a in range(BLOCKS)]
 
@@ -82,7 +83,7 @@ def tile_scatter_matmul_kernel(tc, base, x, w, s, b, offs, out):
             for r in range(EACH):
                 nc.tensor.matmul(
                     window_tiles[EACH * h + r][:].indirect(offsets[:]),
-                    w_blocks[h][:, r, :],
+                    weights[h][:, r, :],
                     x_tile[:],
                     start=True,
                     stop=True,
@@ -90,11 +91,11 @@ def tile_scatter_matmul_kernel(tc, base, x, w, s, b, offs, out):
 
             for r in range(EACH):
                 a = EACH * h + r
-                gain, shift = gains[h][:, r : r + 1], shifts[h][:, r : r + 1]
+                gain, shift = gains[h][:, r, :], shifts[h][:, r, :]
                 result = held.tile([P, S], F32, name=f"result{a}", align_bytes=BURST)
                 if r == 0:
                     nc.scalar.activation(result[:], window_tiles[a][:], IDENTITY, bias=shift, scale=gain)
-                    nc.scalar.dma_start(out_rows[:, h, r, :], result[:])
+                    nc.scalar.dma_start(out_rows[h][:, r, :], result[:])
                 else:
                     nc.vector.tensor_scalar(result[:], window_tiles[a][:], gain, shift, MULT, ADD)
-                    nc.sync.dma_start(out_rows[:, h, r, :], result[:])
+                    nc.sync.dma_start(out_rows[h][:, r, :], result[:])

@@ -13,7 +13,7 @@ BLOCKS = M // P
 HALVES = 2
 EACH = BLOCKS // HALVES
 BURST = 256
-WARM_MATMULS = 12
+WARM_MATMULS = 8
 PIECE = 44
 
 FLOPS = 2 * P * M * N

@@ -94,8 +94,8 @@ def tile_scatter_matmul_kernel(tc, base, x, w, s, b, offs, out):
                 gain, shift = gains[h][:, r, :], shifts[h][:, r, :]
                 result = held.tile([P, S], F32, name=f"result{a}", align_bytes=BURST)
                 if r == 0:
-                    nc.scalar.activation(result[:], window_tiles[a][:], IDENTITY, bias=shift, scale=gain)
-                    nc.scalar.dma_start(out_rows[h][:, r, :], result[:])
-                else:
                     nc.vector.tensor_scalar(result[:], window_tiles[a][:], gain, shift, MULT, ADD)
                     nc.sync.dma_start(out_rows[h][:, r, :], result[:])
+                else:
+                    nc.scalar.activation(result[:], window_tiles[a][:], IDENTITY, bias=shift, scale=gain)
+                    nc.scalar.dma_start(out_rows[h][:, r, :], result[:])

import concourse.mybir as mybir
from concourse.masks import make_identity

BF16, F32, U16 = mybir.dt.bfloat16, mybir.dt.float32, mybir.dt.uint16
MULT, ADD = mybir.AluOpType.mult, mybir.AluOpType.add
IDENTITY = mybir.ActivationFunctionType.Identity

P = 128
S = 512
M = 512
N = 128
BLOCKS = M // P
HALVES = 2
EACH = BLOCKS // HALVES
BURST = 256
WARM_MATMULS = 8
PIECE = 44

FLOPS = 2 * P * M * N


def tile_scatter_matmul_kernel(tc, base, x, w, s, b, offs, out):
    nc = tc.nc
    def rows_of_halves(tensor):
        return (
            tensor[0 : M // HALVES, :].rearrange("(p r) t -> p r t", r=EACH),
            tensor[M // HALVES : M, :].rearrange("(r p) t -> p r t", r=EACH),
        )

    base_rows, out_rows, s_rows, b_rows = [rows_of_halves(tensor) for tensor in (base, out, s, b)]
    with (
        tc.tile_pool(name="held", bufs=1) as held,
        tc.psum_pool(name="windows", bufs=1) as windows,
    ):
        zeros = held.tile([P, P], BF16, name="zeros")
        nc.vector.memset(zeros[:], 0.0)
        unread_bank = windows.tile([P, P], F32, name="unread_bank")
        for i in range(WARM_MATMULS):
            nc.tensor.matmul(unread_bank[:], zeros[:], zeros[:], start=True, stop=True)

        base_tiles = [held.tile([P, EACH, S], BF16, name=f"base_half{h}", align_bytes=BURST) for h in range(HALVES)]
        w_tiles = [held.tile([P, EACH * P], BF16, name=f"w_half{h}", align_bytes=BURST) for h in range(HALVES)]
        x_tile = held.tile([P, N], BF16, name="x_tile", align_bytes=BURST)
        offsets = held.tile([P, N // 16], U16, name="offsets")
        gains = [held.tile([P, EACH, 1], F32, name=f"gain{h}") for h in range(HALVES)]
        shifts = [held.tile([P, EACH, 1], F32, name=f"shift{h}") for h in range(HALVES)]
        nc.sync.dma_start(base_tiles[0][:, 0, :], base_rows[0][:, 0, :])
        nc.sync.dma_start(w_tiles[0][:], w[:, 0 : EACH * P])
        nc.sync.dma_start(base_tiles[0][:, 1, :], base_rows[0][:, 1, :])
        nc.sync.dma_start(offsets[:], offs)
        nc.sync.dma_start(x_tile[:], x)
        nc.sync.dma_start(gains[0][:], s_rows[0])
        nc.sync.dma_start(shifts[0][:], b_rows[0])
        nc.sync.dma_start(base_tiles[1][:], base_rows[1])
        nc.sync.dma_start(w_tiles[1][:], w[:, EACH * P : M])
        nc.sync.dma_start(gains[1][:], s_rows[1])
        nc.sync.dma_start(shifts[1][:], b_rows[1])

        ident = held.tile([P, P], BF16, name="ident")
        make_identity(nc, ident[:])

        one_column = held.tile([P, 1], F32, name="one_column")
        nc.vector.memset(one_column[:], 0.0)
        unread = held.tile([P, 1], F32, name="unread")
        nc.scalar.activation(unread[:], one_column[:], IDENTITY)

        w_regrouped = held.tile([P, EACH, P], BF16, name="w_regrouped")
        nc.vector.tensor_copy(w_regrouped[:], w_tiles[0][:].rearrange("k (p r) -> k r p", r=EACH))
        weights = (w_regrouped, w_tiles[1][:].rearrange("k (r p) -> k r p", r=EACH))

        window_tiles = [windows.tile([P, S], F32, name=f"window{a}") for a in range(BLOCKS)]

        for h in range(HALVES):
            width = S if h == 0 else PIECE
            for r in range(EACH):
                a = EACH * h + r
                for start in range(0, S, width):
                    end = min(start + width, S)
                    nc.tensor.matmul(
                        window_tiles[a][:, start:end], ident[:], base_tiles[h][:, r, start:end], start=True, stop=True
                    )

            for r in range(EACH):
                nc.tensor.matmul(
                    window_tiles[EACH * h + r][:].indirect(offsets[:]),
                    weights[h][:, r, :],
                    x_tile[:],
                    start=True,
                    stop=True,
                )

            for r in range(EACH):
                a = EACH * h + r
                gain, shift = gains[h][:, r, :], shifts[h][:, r, :]
                result = held.tile([P, S], F32, name=f"result{a}", align_bytes=BURST)
                if r == 0:
                    nc.vector.tensor_scalar(result[:], window_tiles[a][:], gain, shift, MULT, ADD)
                    nc.sync.dma_start(out_rows[h][:, r, :], result[:])
                else:
                    nc.scalar.activation(result[:], window_tiles[a][:], IDENTITY, bias=shift, scale=gain)
                    nc.scalar.dma_start(out_rows[h][:, r, :], result[:])
